import numpy as np
import ml_dtypes

BF16 = ml_dtypes.bfloat16


def bf(x):
    return np.asarray(x, np.float32).astype(BF16)


def f32(x):
    return np.asarray(x, np.float32)


def f64(x):
    return np.asarray(x).astype(np.float64)


def striped(idx):
    return np.tile(idx.reshape(-1, 16).T, (8, 1))


S, K, M, N = 4096, 128, 512, 1536


def setup_inputs():
    return {"table": bf(np.random.standard_normal((K, S))), "w": bf(np.random.standard_normal((K, M)) / np.sqrt(K)), "b": f32(0.5 * np.random.standard_normal((M, 1))), "offs": striped(np.random.permutation(np.tile(np.arange(S), 2))[:N])}


def reference(table, w, b, offs):
    idx = offs[:16].T.reshape(-1)
    x = f64(table)[:, idx]
    y = f64(w).T @ x
    return np.tanh(y + f64(b))

@@ -1,0 +1,43 @@
+import concourse.mybir as mybir
+
+BF16, F32, U16 = mybir.dt.bfloat16, mybir.dt.float32, mybir.dt.uint16
+TANH = mybir.ActivationFunctionType.Tanh
+
+P = 128
+WORDS = 4096
+M = 512
+N = 1536
+PIECE = 512
+M_BLOCKS = M // P
+PIECES = N // PIECE
+PIECE_COLS = PIECE // 16
+
+FLOPS = 2 * P * M * N
+
+
+def tile_gather_matmul_kernel(tc, table, w, b, offs, out):
+    nc = tc.nc
+    with (
+        tc.tile_pool(name="held", bufs=1) as held,
+        tc.tile_pool(name="results", bufs=M_BLOCKS) as results,
+        tc.psum_pool(name="banks", bufs=4) as banks,
+    ):
+        offsets = held.tile([P, N // 16], U16, name="offsets")
+        nc.sync.dma_start(offsets[:], offs)
+        words = held.tile([P, WORDS], BF16, name="words")
+        nc.sync.dma_start(words[:], table)
+        weights = held.tile([P, M], BF16, name="weights")
+        nc.scalar.dma_start(weights[:], w)
+        bias = held.tile([P, M_BLOCKS], F32, name="bias")
+        with nc.allow_non_contiguous_dma(reason="one float32 to a partition, 512 in all"):
+            nc.scalar.dma_start(bias[:], b.rearrange("(a p) o -> p (a o)", p=P))
+
+        for a in range(M_BLOCKS):
+            result = results.tile([P, N], F32, name="result")
+            for q in range(PIECES):
+                columns = slice(q * PIECE, (q + 1) * PIECE)
+                picked = words[:].indirect(offsets[:, q * PIECE_COLS : (q + 1) * PIECE_COLS])
+                bank = banks.tile([P, PIECE], F32, name="bank")
+                nc.tensor.matmul(bank[:], weights[:, a * P : (a + 1) * P], picked, start=True, stop=True)
+                nc.scalar.activation(result[:, columns], bank[:], TANH, bias=bias[:, a : a + 1])
+                nc.sync.dma_start(out[a * P : (a + 1) * P, columns], result[:, columns])

@@ -12,6 +12,8 @@ M_BLOCKS = M // P
 PIECES = N // PIECE
 PIECE_COLS = PIECE // 16
 
+WARM_UPS = 8
+
 FLOPS = 2 * P * M * N
 
 
@@ -21,16 +23,30 @@ def tile_gather_matmul_kernel(tc, table, w, b, offs, out):
         tc.tile_pool(name="held", bufs=1) as held,
         tc.tile_pool(name="results", bufs=M_BLOCKS) as results,
         tc.psum_pool(name="banks", bufs=4) as banks,
+        tc.psum_pool(name="idle", bufs=1) as idle,
     ):
         offsets = held.tile([P, N // 16], U16, name="offsets")
         nc.sync.dma_start(offsets[:], offs)
         words = held.tile([P, WORDS], BF16, name="words")
-        nc.sync.dma_start(words[:], table)
+        half = WORDS // 2
+        nc.scalar.dma_start(words[:, :half], table[:, :half])
+        nc.sync.dma_start(words[:, half:], table[:, half:])
         weights = held.tile([P, M], BF16, name="weights")
-        nc.scalar.dma_start(weights[:], w)
+        nc.gpsimd.dma_start(weights[:], w)
         bias = held.tile([P, M_BLOCKS], F32, name="bias")
         with nc.allow_non_contiguous_dma(reason="one float32 to a partition, 512 in all"):
-            nc.scalar.dma_start(bias[:], b.rearrange("(a p) o -> p (a o)", p=P))
+            nc.gpsimd.dma_start(bias[:], b.rearrange("(a p) o -> p (a o)", p=P))
+
+        zeros = held.tile([P, 1], F32, name="zeros")
+        nc.vector.memset(zeros[:], 0.0)
+        unused = held.tile([P, 1], F32, name="unused")
+        nc.scalar.activation(unused[:], zeros[:], TANH)
+
+        nothing = held.tile([P, PIECE], BF16, name="nothing")
+        nc.vector.memset(nothing[:], 0.0)
+        unread = idle.tile([P, PIECE], F32, name="unread")
+        for i in range(WARM_UPS):
+            nc.tensor.matmul(unread[:], nothing[:, :P], nothing[:], start=True, stop=True)
 
         for a in range(M_BLOCKS):
             result = results.tile([P, N], F32, name="result")

@@ -13,6 +13,7 @@ PIECES = N // PIECE
 PIECE_COLS = PIECE // 16
 
 WARM_UPS = 8
+ROW_START = 256
 
 FLOPS = 2 * P * M * N
 
@@ -27,7 +28,7 @@ def tile_gather_matmul_kernel(tc, table, w, b, offs, out):
     ):
         offsets = held.tile([P, N // 16], U16, name="offsets")
         nc.sync.dma_start(offsets[:], offs)
-        words = held.tile([P, WORDS], BF16, name="words")
+        words = held.tile([P, WORDS], BF16, name="words", align_bytes=ROW_START)
         half = WORDS // 2
         nc.scalar.dma_start(words[:, :half], table[:, :half])
         nc.sync.dma_start(words[:, half:], table[:, half:])
@@ -49,7 +50,7 @@ def tile_gather_matmul_kernel(tc, table, w, b, offs, out):
             nc.tensor.matmul(unread[:], nothing[:, :P], nothing[:], start=True, stop=True)
 
         for a in range(M_BLOCKS):
-            result = results.tile([P, N], F32, name="result")
+            result = results.tile([P, N], F32, name="result", align_bytes=ROW_START)
             for q in range(PIECES):
                 columns = slice(q * PIECE, (q + 1) * PIECE)
                 picked = words[:].indirect(offsets[:, q * PIECE_COLS : (q + 1) * PIECE_COLS])

@@ -12,7 +12,6 @@ M_BLOCKS = M // P
 PIECES = N // PIECE
 PIECE_COLS = PIECE // 16
 
-WARM_UPS = 8
 ROW_START = 256
 
 FLOPS = 2 * P * M * N
@@ -24,7 +23,6 @@ def tile_gather_matmul_kernel(tc, table, w, b, offs, out):
         tc.tile_pool(name="held", bufs=1) as held,
         tc.tile_pool(name="results", bufs=M_BLOCKS) as results,
         tc.psum_pool(name="banks", bufs=4) as banks,
-        tc.psum_pool(name="idle", bufs=1) as idle,
     ):
         offsets = held.tile([P, N // 16], U16, name="offsets")
         nc.sync.dma_start(offsets[:], offs)
@@ -42,12 +40,6 @@ def tile_gather_matmul_kernel(tc, table, w, b, offs, out):
         nc.vector.memset(zeros[:], 0.0)
         unused = held.tile([P, 1], F32, name="unused")
         nc.scalar.activation(unused[:], zeros[:], TANH)
-
-        nothing = held.tile([P, PIECE], BF16, name="nothing")
-        nc.vector.memset(nothing[:], 0.0)
-        unread = idle.tile([P, PIECE], F32, name="unread")
-        for i in range(WARM_UPS):
-            nc.tensor.matmul(unread[:], nothing[:, :P], nothing[:], start=True, stop=True)
 
         for a in range(M_BLOCKS):
             result = results.tile([P, N], F32, name="result", align_bytes=ROW_START)

import concourse.mybir as mybir

BF16, F32, U16 = mybir.dt.bfloat16, mybir.dt.float32, mybir.dt.uint16
TANH = mybir.ActivationFunctionType.Tanh

P = 128
WORDS = 4096
M = 512
N = 1536
PIECE = 512
M_BLOCKS = M // P
PIECES = N // PIECE
PIECE_COLS = PIECE // 16

ROW_START = 256

FLOPS = 2 * P * M * N


def tile_gather_matmul_kernel(tc, table, w, b, offs, out):
    nc = tc.nc
    with (
        tc.tile_pool(name="held", bufs=1) as held,
        tc.tile_pool(name="results", bufs=M_BLOCKS) as results,
        tc.psum_pool(name="banks", bufs=4) as banks,
    ):
        offsets = held.tile([P, N // 16], U16, name="offsets")
        nc.sync.dma_start(offsets[:], offs)
        words = held.tile([P, WORDS], BF16, name="words", align_bytes=ROW_START)
        half = WORDS // 2
        nc.scalar.dma_start(words[:, :half], table[:, :half])
        nc.sync.dma_start(words[:, half:], table[:, half:])
        weights = held.tile([P, M], BF16, name="weights")
        nc.gpsimd.dma_start(weights[:], w)
        bias = held.tile([P, M_BLOCKS], F32, name="bias")
        with nc.allow_non_contiguous_dma(reason="one float32 to a partition, 512 in all"):
            nc.gpsimd.dma_start(bias[:], b.rearrange("(a p) o -> p (a o)", p=P))

        zeros = held.tile([P, 1], F32, name="zeros")
        nc.vector.memset(zeros[:], 0.0)
        unused = held.tile([P, 1], F32, name="unused")
        nc.scalar.activation(unused[:], zeros[:], TANH)

        for a in range(M_BLOCKS):
            result = results.tile([P, N], F32, name="result", align_bytes=ROW_START)
            for q in range(PIECES):
                columns = slice(q * PIECE, (q + 1) * PIECE)
                picked = words[:].indirect(offsets[:, q * PIECE_COLS : (q + 1) * PIECE_COLS])
                bank = banks.tile([P, PIECE], F32, name="bank")
                nc.tensor.matmul(bank[:], weights[:, a * P : (a + 1) * P], picked, start=True, stop=True)
                nc.scalar.activation(result[:, columns], bank[:], TANH, bias=bias[:, a : a + 1])
                nc.sync.dma_start(out[a * P : (a + 1) * P, columns], result[:, columns])
